import numpy as np
import ml_dtypes


def mxq(x, axis, fmt="e4m3"):
    dtype, down = {"e4m3": (ml_dtypes.float8_e4m3fn, 7), "e5m2": (ml_dtypes.float8_e5m2, 14)}[fmt]
    v = np.moveaxis(np.asarray(x, np.float32).astype(ml_dtypes.bfloat16).astype(np.float64), axis, -1)
    blocks = v.reshape(v.shape[:-1] + (-1, 32))
    amax = np.abs(blocks).max(-1, keepdims=True)
    byte = np.maximum(np.where(amax > 0, np.frexp(amax)[1] - 1 + 127, 0) - down, 1)
    scale = np.exp2(byte - 127.0)
    codes = (blocks / scale).astype(np.float32).astype(dtype).astype(np.float64)
    return np.moveaxis((codes * scale).reshape(v.shape), -1, axis)


WIDE = False


def mx_kscale(k):
    if not WIDE:
        return np.ones(k)
    levels = np.array([10, -10, 5, -5, 0])
    if k % 512:
        return np.exp2(np.random.permutation(np.resize(levels, k // 32))).repeat(32)
    a = np.empty((k // 512, 16))
    for p in range(k // 512):
        a[p, :8] = np.random.permutation(np.resize(levels, 8))
        for g in range(8):
            far = levels[np.abs(levels - a[p, g]) >= 10]
            a[p, g + 8] = far[np.random.randint(len(far))]
    return np.exp2(a.ravel()).repeat(32)


def f64(x):
    return np.asarray(x).astype(np.float64)


def striped(idx):
    return np.tile(np.asarray(idx).reshape(-1, 16).T, (8, 1)).astype(np.uint16)


def unstriped(offs):
    return offs[:16].T.reshape(-1).astype(np.int64)


B, N, T, D, DV, NQ = 1, 512, 1024, 512, 256, 256


def setup_inputs():
    n = np.random.standard_normal
    idx = np.sort(np.random.permutation(T)[:B * N].reshape(B, N), axis=1).reshape(-1)
    s = mx_kscale(D)[:, None]
    u = np.ones(T)
    u[idx] = mx_kscale(B * N)
    r = np.random.uniform(0.5, 2.0, T)
    rk = np.random.uniform(0.5, 2.0, T)
    k = n((D, T)) / s / rk
    v = n((DV, T)) / (u * r)
    return {
        "qT": (n((B, D, NQ)) * s * (0.60 / np.sqrt(D))).astype(np.float32),
        "kT": k.astype(np.float32),
        "vT": v.astype(np.float32),
        "ks": np.tile(rk, (128, 1)).astype(np.float32),
        "vs": np.tile(u * r, (128, 1)).astype(np.float32),
        "kb": np.tile(n(T), (128, 1)).astype(np.float32),
        "offs": striped(idx),
    }


def reference(qT, kT, vT, ks, vs, kb, offs):
    idx = unstriped(offs)
    k = f64(kT)
    v = f64(vT)
    pick = lambda x: x[:, idx].reshape(x.shape[0], B, N).transpose(1, 0, 2)
    q = f64(qT)
    score = mxq(q, 1, "e4m3").transpose(0, 2, 1) @ mxq(pick(k), 1, "e4m3")
    score = score * pick(f64(ks))[:, :1, :]
    score = score + pick(f64(kb))[:, :1, :]
    m = score.max(-1, keepdims=True)
    p = np.exp(score - m)
    total = p.sum(-1, keepdims=True)
    w = p * pick(f64(vs))[:, :1, :]
    y = mxq(w, 2, "e4m3") @ mxq(pick(v).transpose(0, 2, 1), 1, "e4m3")
    y = y / total
    return y

@@ -1,0 +1,199 @@
+from contextlib import ExitStack
+
+import concourse.mybir as mybir
+from concourse.masks import make_identity
+
+P = 128
+D, T, N, NQ, DV = 512, 1024, 512, 256, 256
+F32 = mybir.dt.float32
+BF16 = mybir.dt.bfloat16
+U32 = mybir.dt.uint32
+U16 = mybir.dt.uint16
+U8 = mybir.dt.uint8
+FP8X4 = mybir.dt.float8_e4m3fn_x4
+ACT = mybir.ActivationFunctionType
+ALU = mybir.AluOpType
+AX = mybir.AxisListType
+
+FLOPS = 2 * NQ * N * (D + DV)
+BYTES = 4 * (D * NQ + (D + DV) * N + 3 * N + NQ * DV) + 2 * N
+
+
+def tile_attend_x_ks_bias_srt_kernel(tc, qT, kT, vT, ks, vs, kb, offs, out):
+    nc = tc.nc
+    with ExitStack() as ctx:
+        keep = ctx.enter_context(tc.tile_pool(name="keep", bufs=1))
+        psum = ctx.enter_context(tc.psum_pool(name="psum", bufs=2))
+
+        offsets = keep.tile([P, N // 16], U16, name="offsets")
+        ks_row = keep.tile([P, T], F32, name="ks_row")
+        kb_row = keep.tile([P, T], F32, name="kb_row")
+        vs_row = keep.tile([P, T], F32, name="vs_row")
+        warm = keep.tile([P, 1], F32, name="warm")
+        ident = keep.tile([P, P], F32, name="ident")
+
+        nc.sync.dma_start(offsets[:], offs)
+        nc.gpsimd.memset(ks_row[:], 0.0)
+        nc.vector.memset(warm[:], 0.0)
+        nc.vector.memset(kb_row[:], 0.0)
+        nc.gpsimd.memset(vs_row[:], 0.0)
+        nc.scalar.activation(out=warm[:], in_=warm[:], func=ACT.Exp)
+        make_identity(nc, ident[:])
+
+        H = T // 2
+        k_view = kT.rearrange("(p j) n -> p j n", j=4)
+        k_raw = {}
+
+        def load_k(u, h):
+            k_raw[u, h] = keep.tile([P, 2, H], F32, name=f"k_raw{u}{h}")
+            nc.sync.dma_start(k_raw[u, h][:], k_view[:, 2 * u : 2 * u + 2, h * H : (h + 1) * H])
+
+        load_k(0, 0)
+        nc.sync.dma_start(ks_row[0:1, :], ks[0:1, :])
+        nc.sync.dma_start(kb_row[0:1, :], kb[0:1, :])
+        load_k(0, 1)
+        nc.sync.dma_start(vs_row[0:1, :], vs[0:1, :])
+        load_k(1, 0)
+        load_k(1, 1)
+        q_raw = keep.tile([P, 4, NQ], F32, name="q_raw")
+        nc.sync.dma_start(q_raw[:], qT[0].rearrange("(p j) n -> p j n", j=4))
+        v_raw = []
+        for h in range(2):
+            t = keep.tile([P, 2, H], F32, name=f"v_raw{h}")
+            nc.sync.dma_start(t[:], vT.rearrange("(p j) n -> p j n", j=2)[:, :, h * H : (h + 1) * H])
+            v_raw.append(t)
+
+        def table_columns(row, step, name, tag):
+            g = keep.tile([P, N], F32, name=name + "_g")
+            nc.vector.tensor_copy(g[:], row[:].indirect(offsets[:]))
+            bank = psum.tile([P, 4, P], F32, name=name + "_t", tag=tag)
+            for c in range(4):
+                src = g[:, c * P : (c + 1) * P] if step == 1 else g[:, c : N : 4]
+                nc.tensor.transpose(bank[:, c, :], src, ident[:])
+            col = keep.tile([P, 4], F32, name=name + "_c")
+            nc.vector.tensor_copy(col[:], bank[:, :, 0])
+            return col
+
+        ks_col = table_columns(ks_row, 1, "ks", "x")
+        kb_col = table_columns(kb_row, 1, "kb", "x")
+
+        k_grp = keep.tile([P, N * 4], BF16, name="k_grp", align_bytes=64)
+        k_words = k_grp[:].bitcast(U32).rearrange("p (i u) -> p i u", u=2)
+        k_pool = []
+        for u in range(2):
+            t = keep.tile([P, T * 2], BF16, name=f"k_pool{u}", align_bytes=64)
+            for h in range(2):
+                nc.scalar.activation(
+                    out=t[:, h * T : (h + 1) * T].rearrange("p (n h) -> p n h", h=2),
+                    in_=k_raw[u, h][:].rearrange("p h n -> p n h"),
+                    func=ACT.Copy,
+                )
+            k_pool.append(t)
+            nc.vector.tensor_copy(k_words[:, :, u], t[:].bitcast(U32).indirect(offsets[:]))
+            if u == 0:
+                vs_col = table_columns(vs_row, 4, "vs", "y")
+
+        q_grp = keep.tile([P, NQ * 4], BF16, name="q_grp", align_bytes=64)
+        nc.gpsimd.tensor_copy(q_grp[:].rearrange("p (n j) -> p n j", j=4), q_raw[:].rearrange("p j n -> p n j"))
+        q_codes = keep.tile([P, NQ], U32, name="q_codes", align_bytes=64)
+        q_scale = keep.tile([P, NQ], U8, name="q_scale", align_bytes=64)
+        k_codes = keep.tile([P, N], U32, name="k_codes", align_bytes=64)
+        k_scale = keep.tile([P, N], U8, name="k_scale", align_bytes=64)
+        nc.vector.quantize_mx(out=k_codes[:].bitcast(FP8X4), scales=k_scale[:], in_=k_grp[:])
+        nc.vector.quantize_mx(out=q_codes[:].bitcast(FP8X4), scales=q_scale[:], in_=q_grp[:])
+
+        s_t = keep.tile([P, 4, NQ], F32, name="s_t")
+        for half in range(2):
+            bank = psum.tile([P, 2, NQ], F32, name="qk", tag="x")
+            for c2 in range(2):
+                c = 2 * half + c2
+                sl = slice(c * P, (c + 1) * P)
+                nc.tensor.matmul_mx(
+                    out=bank[:, c2, :],
+                    lhsT=k_codes[:, sl].bitcast(FP8X4),
+                    lhsT_scale=k_scale[:, sl],
+                    rhs=q_codes[:].bitcast(FP8X4),
+                    rhs_scale=q_scale[:],
+                    start=True,
+                    stop=True,
+                )
+            for c2 in range(2):
+                c = 2 * half + c2
+                nc.scalar.activation(
+                    out=s_t[:, c, :],
+                    in_=bank[:, c2, :],
+                    func=ACT.Identity,
+                    scale=ks_col[:, c : c + 1],
+                    bias=kb_col[:, c : c + 1],
+                )
+
+        v_pool = keep.tile([P, T * 2], BF16, name="v_pool", align_bytes=64)
+        for h in range(2):
+            nc.scalar.activation(
+                out=v_pool[:, h * T : (h + 1) * T].rearrange("p (n h) -> p n h", h=2),
+                in_=v_raw[h][:].rearrange("p h n -> p n h"),
+                func=ACT.Copy,
+            )
+        v_g = keep.tile([P, N], U32, name="v_g", align_bytes=64)
+        nc.vector.tensor_copy(v_g[:], v_pool[:].bitcast(U32).indirect(offsets[:]))
+        v_words = v_g[:].bitcast(F32)
+        v_grp = keep.tile([P, DV * 4], BF16, name="v_grp", align_bytes=64)
+        v_view = v_grp[:].rearrange("p (e t) -> p e t", t=4)
+        v_bank = psum.tile([P, 4, P], F32, name="v_t", tag="z")
+        for t in range(4):
+            nc.tensor.transpose(v_bank[:, t, :], v_words[:, t : N : 4], ident[:])
+        nc.scalar.copy(out=v_view, in_=v_bank[:].rearrange("p t e -> p (t e)").bitcast(BF16).rearrange("p (t e) -> p e t", t=4))
+        v_codes = keep.tile([P, DV], U32, name="v_codes", align_bytes=64)
+        v_scale = keep.tile([P, DV], U8, name="v_scale", align_bytes=64)
+
+        p_tiles = []
+        rl_tiles = []
+        for b in range(2):
+            bank = psum.tile([P, N], F32, name="s_b", tag="y")
+            for c in range(4):
+                nc.tensor.transpose(bank[:, c * P : (c + 1) * P], s_t[:, c, b * P : (b + 1) * P], ident[:])
+            neg_m = keep.tile([P, 1], F32, name=f"neg_m{b}")
+            nc.vector.tensor_reduce(out=neg_m[:], in_=bank[:], axis=AX.X, op=ALU.max, negate=True)
+            p = keep.tile([P, 4, P], F32, name=f"p{b}")
+            l = keep.tile([P, 1], F32, name=f"l{b}")
+            nc.scalar.activation(
+                out=p[:],
+                in_=bank[:].rearrange("p (s t) -> p t s", t=4),
+                func=ACT.Exp,
+                bias=neg_m[:],
+                accum_out=l[:],
+            )
+            rl = keep.tile([P, 1], F32, name=f"rl{b}")
+            p_tiles.append(p)
+            nc.vector.reciprocal(rl[:], l[:])
+            rl_tiles.append(rl)
+
+        nc.vector.quantize_mx(out=v_codes[:].bitcast(FP8X4), scales=v_scale[:], in_=v_grp[:])
+
+        for b in range(2):
+            bank = psum.tile([P, 4, P], F32, name="p_t", tag="x")
+            for t in range(4):
+                nc.tensor.transpose(bank[:, t, :], p_tiles[b][:, t, :], ident[:])
+            w_grp = keep.tile([P, P * 4], BF16, name=f"w_grp{b}", align_bytes=64)
+            nc.vector.tensor_tensor(
+                out=w_grp[:].rearrange("p (q t) -> p q t", t=4),
+                in0=bank[:].rearrange("p t q -> p q t"),
+                in1=vs_col[:].unsqueeze(1).to_broadcast([P, P, 4]),
+                op=ALU.mult,
+            )
+            w_codes = keep.tile([P, P], U32, name=f"w_codes{b}", align_bytes=64)
+            w_scale = keep.tile([P, P], U8, name=f"w_scale{b}", align_bytes=64)
+            nc.vector.quantize_mx(out=w_codes[:].bitcast(FP8X4), scales=w_scale[:], in_=w_grp[:])
+            acc = psum.tile([P, DV], F32, name="acc", tag="w")
+            nc.tensor.matmul_mx(
+                out=acc[:],
+                lhsT=w_codes[:].bitcast(FP8X4),
+                lhsT_scale=w_scale[:],
+                rhs=v_codes[:].bitcast(FP8X4),
+                rhs_scale=v_scale[:],
+                start=True,
+                stop=True,
+            )
+            y = keep.tile([P, DV], F32, name=f"y{b}")
+            nc.scalar.activation(out=y[:], in_=acc[:], func=ACT.Copy, scale=rl_tiles[b][:])
+            nc.sync.dma_start(out[0, b * P : (b + 1) * P, :], y[:])

@@ -33,76 +33,106 @@ def tile_attend_x_ks_bias_srt_kernel(tc, qT, kT, vT, ks, vs, kb, offs, out):
         ident = keep.tile([P, P], F32, name="ident")
 
         nc.sync.dma_start(offsets[:], offs)
-        nc.gpsimd.memset(ks_row[:], 0.0)
-        nc.vector.memset(warm[:], 0.0)
-        nc.vector.memset(kb_row[:], 0.0)
-        nc.gpsimd.memset(vs_row[:], 0.0)
+        nc.gpsimd.memset(warm[:], 0.0)
         nc.scalar.activation(out=warm[:], in_=warm[:], func=ACT.Exp)
+        for row in (ks_row, kb_row, vs_row):
+            nc.gpsimd.memset(row[:, : T // 2], 0.0)
+            nc.vector.memset(row[:, T // 2 :], 0.0)
         make_identity(nc, ident[:])
 
-        H = T // 2
         k_view = kT.rearrange("(p j) n -> p j n", j=4)
-        k_raw = {}
+        k_pool = [keep.tile([P, T * 2], BF16, name=f"k_pool{u}", tag=f"pair{u}", align_bytes=64) for u in range(2)]
 
-        def load_k(u, h):
-            k_raw[u, h] = keep.tile([P, 2, H], F32, name=f"k_raw{u}{h}")
-            nc.sync.dma_start(k_raw[u, h][:], k_view[:, 2 * u : 2 * u + 2, h * H : (h + 1) * H])
+        def load_pair(view, j, lo, hi, name):
+            t = keep.tile([P, 2, hi - lo], F32, name=name, tag=name)
+            nc.sync.dma_start(t[:], view[:, j : j + 2, lo:hi])
+            return t
 
-        load_k(0, 0)
-        nc.sync.dma_start(ks_row[0:1, :], ks[0:1, :])
-        nc.sync.dma_start(kb_row[0:1, :], kb[0:1, :])
-        load_k(0, 1)
-        nc.sync.dma_start(vs_row[0:1, :], vs[0:1, :])
-        load_k(1, 0)
-        load_k(1, 1)
-        q_raw = keep.tile([P, 4, NQ], F32, name="q_raw")
-        nc.sync.dma_start(q_raw[:], qT[0].rearrange("(p j) n -> p j n", j=4))
-        v_raw = []
-        for h in range(2):
-            t = keep.tile([P, 2, H], F32, name=f"v_raw{h}")
-            nc.sync.dma_start(t[:], vT.rearrange("(p j) n -> p j n", j=2)[:, :, h * H : (h + 1) * H])
-            v_raw.append(t)
+        def cast_pair(engine_copy, pool, raw, lo, hi, base):
+            engine_copy(
+                pool[:, 2 * lo : 2 * hi].rearrange("p (n h) -> p n h", h=2),
+                raw[:, :, lo - base : hi - base].rearrange("p h n -> p n h"),
+            )
 
-        def table_columns(row, step, name, tag):
-            g = keep.tile([P, N], F32, name=name + "_g")
+        def scalar_cast(o, i):
+            nc.scalar.activation(out=o, in_=i, func=ACT.Copy)
+
+        def gather_table(row, name):
+            g = keep.tile([P, N], F32, name=name + "_g", tag="pair0" if name == "vs" else name + "_g", align_bytes=64)
             nc.vector.tensor_copy(g[:], row[:].indirect(offsets[:]))
+            return g
+
+        def turn_table(g, step, name, tag):
             bank = psum.tile([P, 4, P], F32, name=name + "_t", tag=tag)
             for c in range(4):
                 src = g[:, c * P : (c + 1) * P] if step == 1 else g[:, c : N : 4]
                 nc.tensor.transpose(bank[:, c, :], src, ident[:])
-            col = keep.tile([P, 4], F32, name=name + "_c")
-            nc.vector.tensor_copy(col[:], bank[:, :, 0])
+            return bank
+
+        def column(bank, name, tag):
+            col = keep.tile([P, 4], F32, name=name + "_c", tag=tag)
+            nc.scalar.activation(out=col[:], in_=bank[:, :, 0], func=ACT.Copy)
             return col
 
-        ks_col = table_columns(ks_row, 1, "ks", "x")
-        kb_col = table_columns(kb_row, 1, "kb", "x")
+        CUT = 512
+        k0a = load_pair(k_view, 0, 0, CUT, "k0a")
+        nc.sync.dma_start(ks_row[0:1, :], ks[0:1, :])
+        nc.sync.dma_start(kb_row[0:1, :], kb[0:1, :])
+        k0b = load_pair(k_view, 0, CUT, T, "k0b")
+        nc.sync.dma_start(vs_row[0:1, :], vs[0:1, :])
+        k1a = load_pair(k_view, 2, 0, 512, "k1a")
+        k1b = load_pair(k_view, 2, 512, T, "k1b")
+        q_raw = keep.tile([P, 4, NQ], F32, name="q_raw", tag="q_raw")
+        nc.sync.dma_start(q_raw[:], qT[0].rearrange("(p j) n -> p j n", j=4))
+        v_raw = []
+        for e in range(2):
+            t = keep.tile([P, T], F32, name=f"v_raw{e}")
+            nc.sync.dma_start(t[:], vT[e * P : (e + 1) * P, :])
+            v_raw.append(t)
 
-        k_grp = keep.tile([P, N * 4], BF16, name="k_grp", align_bytes=64)
+        ks_g = gather_table(ks_row, "ks")
+        ks_bank = turn_table(ks_g, 1, "ks", "x")
+        kb_g = gather_table(kb_row, "kb")
+        kb_bank = turn_table(kb_g, 1, "kb", "x")
+
+        k_grp = keep.tile([P, N * 4], BF16, name="k_grp", tag="k_grp", align_bytes=64)
         k_words = k_grp[:].bitcast(U32).rearrange("p (i u) -> p i u", u=2)
-        k_pool = []
-        for u in range(2):
-            t = keep.tile([P, T * 2], BF16, name=f"k_pool{u}", align_bytes=64)
-            for h in range(2):
-                nc.scalar.activation(
-                    out=t[:, h * T : (h + 1) * T].rearrange("p (n h) -> p n h", h=2),
-                    in_=k_raw[u, h][:].rearrange("p h n -> p n h"),
-                    func=ACT.Copy,
-                )
-            k_pool.append(t)
-            nc.vector.tensor_copy(k_words[:, :, u], t[:].bitcast(U32).indirect(offsets[:]))
-            if u == 0:
-                vs_col = table_columns(vs_row, 4, "vs", "y")
-
-        q_grp = keep.tile([P, NQ * 4], BF16, name="q_grp", align_bytes=64)
-        nc.gpsimd.tensor_copy(q_grp[:].rearrange("p (n j) -> p n j", j=4), q_raw[:].rearrange("p j n -> p n j"))
-        q_codes = keep.tile([P, NQ], U32, name="q_codes", align_bytes=64)
-        q_scale = keep.tile([P, NQ], U8, name="q_scale", align_bytes=64)
         k_codes = keep.tile([P, N], U32, name="k_codes", align_bytes=64)
         k_scale = keep.tile([P, N], U8, name="k_scale", align_bytes=64)
-        nc.vector.quantize_mx(out=k_codes[:].bitcast(FP8X4), scales=k_scale[:], in_=k_grp[:])
+        q_grp = keep.tile([P, NQ * 4], BF16, name="q_grp", align_bytes=64)
+        q_codes = keep.tile([P, NQ], U32, name="q_codes", align_bytes=64)
+        q_scale = keep.tile([P, NQ], U8, name="q_scale", align_bytes=64)
+
+        cast_pair(scalar_cast, k_pool[0], k0a, 0, CUT, 0)
+        cast_pair(scalar_cast, k_pool[0], k0b, CUT, T, CUT)
+        nc.vector.tensor_copy(k_words[:, :, 0], k_pool[0][:].bitcast(U32).indirect(offsets[:]))
+        cast_pair(scalar_cast, k_pool[1], k1a, 0, 512, 0)
+        cast_pair(scalar_cast, k_pool[1], k1b, 512, T, 512)
+        vs_g = gather_table(vs_row, "vs")
+        vs_bank = turn_table(vs_g, 4, "vs", "w")
+        for h in range(2):
+            nc.vector.tensor_copy(
+                k_words[:, h * 256 : (h + 1) * 256, 1],
+                k_pool[1][:].bitcast(U32).indirect(offsets[:, h * 16 : (h + 1) * 16]),
+            )
+        scalar_cast(q_grp[:].rearrange("p (n j) -> p n j", j=4), q_raw[:].rearrange("p j n -> p n j"))
+        ks_col = column(ks_bank, "ks", "k1a")
+        kb_col = column(kb_bank, "kb", "k1b")
+        vs_col = column(vs_bank, "vs", "q_raw")
+
+        def quantize_k(h):
+            nc.vector.quantize_mx(
+                out=k_codes[:, h * 256 : (h + 1) * 256].bitcast(FP8X4),
+                scales=k_scale[:, h * 256 : (h + 1) * 256],
+                in_=k_grp[:, h * 1024 : (h + 1) * 1024],
+            )
+
         nc.vector.quantize_mx(out=q_codes[:].bitcast(FP8X4), scales=q_scale[:], in_=q_grp[:])
+        quantize_k(0)
+        quantize_k(1)
 
         s_t = keep.tile([P, 4, NQ], F32, name="s_t")
+        banks = []
         for half in range(2):
             bank = psum.tile([P, 2, NQ], F32, name="qk", tag="x")
             for c2 in range(2):
@@ -117,58 +147,62 @@ def tile_attend_x_ks_bias_srt_kernel(tc, qT, kT, vT, ks, vs, kb, offs, out):
                     start=True,
                     stop=True,
                 )
-            for c2 in range(2):
-                c = 2 * half + c2
-                nc.scalar.activation(
-                    out=s_t[:, c, :],
-                    in_=bank[:, c2, :],
-                    func=ACT.Identity,
-                    scale=ks_col[:, c : c + 1],
-                    bias=kb_col[:, c : c + 1],
-                )
-
-        v_pool = keep.tile([P, T * 2], BF16, name="v_pool", align_bytes=64)
-        for h in range(2):
+            banks.append(bank)
+        for c in range(4):
             nc.scalar.activation(
-                out=v_pool[:, h * T : (h + 1) * T].rearrange("p (n h) -> p n h", h=2),
-                in_=v_raw[h][:].rearrange("p h n -> p n h"),
-                func=ACT.Copy,
+                out=s_t[:, c, :], in_=banks[c // 2][:, c % 2, :], func=ACT.Identity,
+                scale=ks_col[:, c : c + 1], bias=kb_col[:, c : c + 1],
             )
-        v_g = keep.tile([P, N], U32, name="v_g", align_bytes=64)
-        nc.vector.tensor_copy(v_g[:], v_pool[:].bitcast(U32).indirect(offsets[:]))
-        v_words = v_g[:].bitcast(F32)
+
+        v_g = []
+        for e in range(2):
+            g = keep.tile([P, N], F32, name=f"v_g{e}", tag="pair1" if e == 0 else "k_grp", align_bytes=64)
+            nc.vector.tensor_copy(g[:], v_raw[e][:].indirect(offsets[:]))
+            v_g.append(g)
         v_grp = keep.tile([P, DV * 4], BF16, name="v_grp", align_bytes=64)
-        v_view = v_grp[:].rearrange("p (e t) -> p e t", t=4)
-        v_bank = psum.tile([P, 4, P], F32, name="v_t", tag="z")
-        for t in range(4):
-            nc.tensor.transpose(v_bank[:, t, :], v_words[:, t : N : 4], ident[:])
-        nc.scalar.copy(out=v_view, in_=v_bank[:].rearrange("p t e -> p (t e)").bitcast(BF16).rearrange("p (t e) -> p e t", t=4))
         v_codes = keep.tile([P, DV], U32, name="v_codes", align_bytes=64)
         v_scale = keep.tile([P, DV], U8, name="v_scale", align_bytes=64)
 
-        p_tiles = []
-        rl_tiles = []
+        s_banks = []
         for b in range(2):
             bank = psum.tile([P, N], F32, name="s_b", tag="y")
             for c in range(4):
                 nc.tensor.transpose(bank[:, c * P : (c + 1) * P], s_t[:, c, b * P : (b + 1) * P], ident[:])
+            s_banks.append(bank)
+        v_banks = []
+        for e in range(2):
+            bank = psum.tile([P, 4, P], F32, name="v_t", tag="z")
+            for t in range(4):
+                nc.tensor.transpose(bank[:, t, :], v_g[e][:, t : N : 4], ident[:])
+            v_banks.append(bank)
+
+        def value_copy(engine_copy, e):
+            engine_copy(
+                v_grp[:, e * 512 : (e + 1) * 512].rearrange("p (e t) -> p e t", t=4),
+                v_banks[e][:].rearrange("p t e -> p e t"),
+            )
+
+        value_copy(scalar_cast, 0)
+        neg_ms = []
+        for b in range(2):
             neg_m = keep.tile([P, 1], F32, name=f"neg_m{b}")
-            nc.vector.tensor_reduce(out=neg_m[:], in_=bank[:], axis=AX.X, op=ALU.max, negate=True)
+            nc.vector.tensor_reduce(out=neg_m[:], in_=s_banks[b][:], axis=AX.X, op=ALU.max, negate=True)
+            neg_ms.append(neg_m)
+        p_tiles = []
+        l_tiles = []
+        for b in range(2):
             p = keep.tile([P, 4, P], F32, name=f"p{b}")
             l = keep.tile([P, 1], F32, name=f"l{b}")
             nc.scalar.activation(
                 out=p[:],
-                in_=bank[:].rearrange("p (s t) -> p t s", t=4),
+                in_=s_banks[b][:].rearrange("p (s t) -> p t s", t=4),
                 func=ACT.Exp,
-                bias=neg_m[:],
+                bias=neg_ms[b][:],
                 accum_out=l[:],
             )
-            rl = keep.tile([P, 1], F32, name=f"rl{b}")
             p_tiles.append(p)
-            nc.vector.reciprocal(rl[:], l[:])
-            rl_tiles.append(rl)
-
-        nc.vector.quantize_mx(out=v_codes[:].bitcast(FP8X4), scales=v_scale[:], in_=v_grp[:])
+            l_tiles.append(l)
+        value_copy(nc.vector.tensor_copy, 1)
 
         for b in range(2):
             bank = psum.tile([P, 4, P], F32, name="p_t", tag="x")
@@ -184,6 +218,10 @@ def tile_attend_x_ks_bias_srt_kernel(tc, qT, kT, vT, ks, vs, kb, offs, out):
             w_codes = keep.tile([P, P], U32, name=f"w_codes{b}", align_bytes=64)
             w_scale = keep.tile([P, P], U8, name=f"w_scale{b}", align_bytes=64)
             nc.vector.quantize_mx(out=w_codes[:].bitcast(FP8X4), scales=w_scale[:], in_=w_grp[:])
+            if b == 0:
+                nc.vector.quantize_mx(out=v_codes[:].bitcast(FP8X4), scales=v_scale[:], in_=v_grp[:])
+            rl = keep.tile([P, 1], F32, name=f"rl{b}")
+            nc.vector.reciprocal(rl[:], l_tiles[b][:])
             acc = psum.tile([P, DV], F32, name="acc", tag="w")
             nc.tensor.matmul_mx(
                 out=acc[:],
@@ -195,5 +233,5 @@ def tile_attend_x_ks_bias_srt_kernel(tc, qT, kT, vT, ks, vs, kb, offs, out):
                 stop=True,
             )
             y = keep.tile([P, DV], F32, name=f"y{b}")
-            nc.scalar.activation(out=y[:], in_=acc[:], func=ACT.Copy, scale=rl_tiles[b][:])
+            nc.scalar.activation(out=y[:], in_=acc[:], func=ACT.Copy, scale=rl[:])
             nc.sync.dma_start(out[0, b * P : (b + 1) * P, :], y[:])

@@ -31,21 +31,23 @@ def tile_attend_x_ks_bias_srt_kernel(tc, qT, kT, vT, ks, vs, kb, offs, out):
         vs_row = keep.tile([P, T], F32, name="vs_row")
         warm = keep.tile([P, 1], F32, name="warm")
         ident = keep.tile([P, P], F32, name="ident")
+        ident_bf16 = keep.tile([P, P], BF16, name="ident_bf16")
 
         nc.sync.dma_start(offsets[:], offs)
-        nc.gpsimd.memset(warm[:], 0.0)
+        nc.vector.memset(warm[:], 0.0)
         nc.scalar.activation(out=warm[:], in_=warm[:], func=ACT.Exp)
-        for row in (ks_row, kb_row, vs_row):
-            nc.gpsimd.memset(row[:, : T // 2], 0.0)
-            nc.vector.memset(row[:, T // 2 :], 0.0)
+        for row, cut in ((ks_row, 808), (kb_row, 512), (vs_row, 384)):
+            nc.gpsimd.memset(row[:, :cut], 0.0)
+            nc.vector.memset(row[:, cut:], 0.0)
         make_identity(nc, ident[:])
+        make_identity(nc, ident_bf16[:])
 
         k_view = kT.rearrange("(p j) n -> p j n", j=4)
-        k_pool = [keep.tile([P, T * 2], BF16, name=f"k_pool{u}", tag=f"pair{u}", align_bytes=64) for u in range(2)]
+        k_pool = [keep.tile([P, T * 2], BF16, name=f"k_pool{u}", align_bytes=64) for u in range(2)]
 
-        def load_pair(view, j, lo, hi, name):
+        def load_pair(j, lo, hi, name):
             t = keep.tile([P, 2, hi - lo], F32, name=name, tag=name)
-            nc.sync.dma_start(t[:], view[:, j : j + 2, lo:hi])
+            nc.sync.dma_start(t[:], k_view[:, j : j + 2, lo:hi])
             return t
 
         def cast_pair(engine_copy, pool, raw, lo, hi, base):
@@ -57,10 +59,8 @@ def tile_attend_x_ks_bias_srt_kernel(tc, qT, kT, vT, ks, vs, kb, offs, out):
         def scalar_cast(o, i):
             nc.scalar.activation(out=o, in_=i, func=ACT.Copy)
 
-        def gather_table(row, name):
-            g = keep.tile([P, N], F32, name=name + "_g", tag="pair0" if name == "vs" else name + "_g", align_bytes=64)
-            nc.vector.tensor_copy(g[:], row[:].indirect(offsets[:]))
-            return g
+        def gather_table(row, g):
+            nc.vector.tensor_copy(g, row[:].indirect(offsets[:]))
 
         def turn_table(g, step, name, tag):
             bank = psum.tile([P, 4, P], F32, name=name + "_t", tag=tag)
@@ -74,94 +74,92 @@ def tile_attend_x_ks_bias_srt_kernel(tc, qT, kT, vT, ks, vs, kb, offs, out):
             nc.scalar.activation(out=col[:], in_=bank[:, :, 0], func=ACT.Copy)
             return col
 
-        CUT = 512
-        k0a = load_pair(k_view, 0, 0, CUT, "k0a")
+        def keep_tensor_engine_awake(blocks, tags):
+            for tag in tags:
+                bank = psum.tile([P, 4, P], F32, name="awake", tag=tag)
+                for i in range(4):
+                    nc.tensor.transpose(bank[:, i, :], blocks[:, i * P : (i + 1) * P], ident[:])
+
+        k0a = load_pair(0, 0, 512, "k0a")
         nc.sync.dma_start(ks_row[0:1, :], ks[0:1, :])
+        k0b = load_pair(0, 512, T, "k0b")
         nc.sync.dma_start(kb_row[0:1, :], kb[0:1, :])
-        k0b = load_pair(k_view, 0, CUT, T, "k0b")
-        nc.sync.dma_start(vs_row[0:1, :], vs[0:1, :])
-        k1a = load_pair(k_view, 2, 0, 512, "k1a")
-        k1b = load_pair(k_view, 2, 512, T, "k1b")
+        k1a = load_pair(2, 0, 512, "k1a")
+        k1b = load_pair(2, 512, T, "k1b")
         q_raw = keep.tile([P, 4, NQ], F32, name="q_raw", tag="q_raw")
         nc.sync.dma_start(q_raw[:], qT[0].rearrange("(p j) n -> p j n", j=4))
+        nc.sync.dma_start(vs_row[0:1, :], vs[0:1, :])
         v_raw = []
         for e in range(2):
             t = keep.tile([P, T], F32, name=f"v_raw{e}")
             nc.sync.dma_start(t[:], vT[e * P : (e + 1) * P, :])
             v_raw.append(t)
 
-        ks_g = gather_table(ks_row, "ks")
-        ks_bank = turn_table(ks_g, 1, "ks", "x")
-        kb_g = gather_table(kb_row, "kb")
-        kb_bank = turn_table(kb_g, 1, "kb", "x")
+        tab_g = keep.tile([P, 2, N], F32, name="tab_g", align_bytes=64)
+        gather_table(ks_row, tab_g[:, 0, :])
+        ks_bank = turn_table(tab_g[:, 0, :], 1, "ks", "x")
+        gather_table(kb_row, tab_g[:, 1, :])
+        kb_bank = turn_table(tab_g[:, 1, :], 1, "kb", "x")
 
-        k_grp = keep.tile([P, N * 4], BF16, name="k_grp", tag="k_grp", align_bytes=64)
-        k_words = k_grp[:].bitcast(U32).rearrange("p (i u) -> p i u", u=2)
-        k_codes = keep.tile([P, N], U32, name="k_codes", align_bytes=64)
-        k_scale = keep.tile([P, N], U8, name="k_scale", align_bytes=64)
-        q_grp = keep.tile([P, NQ * 4], BF16, name="q_grp", align_bytes=64)
-        q_codes = keep.tile([P, NQ], U32, name="q_codes", align_bytes=64)
-        q_scale = keep.tile([P, NQ], U8, name="q_scale", align_bytes=64)
+        keep_tensor_engine_awake(k1a[:, 0, :], "yz")
+        keep_tensor_engine_awake(q_raw[:].rearrange("p j n -> p (j n)"), "yzyz")
 
-        cast_pair(scalar_cast, k_pool[0], k0a, 0, CUT, 0)
-        cast_pair(scalar_cast, k_pool[0], k0b, CUT, T, CUT)
+        grp = keep.tile([P, (NQ + N) * 4], BF16, name="grp", tag="grp", align_bytes=64)
+        codes = keep.tile([P, NQ + N], U32, name="codes", align_bytes=64)
+        scales = keep.tile([P, NQ + N], U8, name="scales", align_bytes=64)
+        k_words = grp[:, NQ * 4 :].bitcast(U32).rearrange("p (i u) -> p i u", u=2)
+
+        cast_pair(scalar_cast, k_pool[0], k0a, 0, 512, 0)
+        cast_pair(scalar_cast, k_pool[0], k0b, 512, T, 512)
         nc.vector.tensor_copy(k_words[:, :, 0], k_pool[0][:].bitcast(U32).indirect(offsets[:]))
         cast_pair(scalar_cast, k_pool[1], k1a, 0, 512, 0)
-        cast_pair(scalar_cast, k_pool[1], k1b, 512, T, 512)
-        vs_g = gather_table(vs_row, "vs")
-        vs_bank = turn_table(vs_g, 4, "vs", "w")
+        cast_pair(scalar_cast, k_pool[1], k1b, 512, 704, 512)
+        cast_pair(nc.vector.tensor_copy, k_pool[1], k1b, 704, T, 512)
         for h in range(2):
             nc.vector.tensor_copy(
                 k_words[:, h * 256 : (h + 1) * 256, 1],
                 k_pool[1][:].bitcast(U32).indirect(offsets[:, h * 16 : (h + 1) * 16]),
             )
-        scalar_cast(q_grp[:].rearrange("p (n j) -> p n j", j=4), q_raw[:].rearrange("p j n -> p n j"))
+        q_half = NQ // 2
+        for engine_copy, lo in ((scalar_cast, 0), (nc.gpsimd.tensor_copy, q_half)):
+            engine_copy(
+                grp[:, 4 * lo : 4 * (lo + q_half)].rearrange("p (n j) -> p n j", j=4),
+                q_raw[:, :, lo : lo + q_half].rearrange("p j n -> p n j"),
+            )
         ks_col = column(ks_bank, "ks", "k1a")
         kb_col = column(kb_bank, "kb", "k1b")
-        vs_col = column(vs_bank, "vs", "q_raw")
-
-        def quantize_k(h):
+        v_pool0 = keep.tile([P, T], BF16, name="v_pool0", align_bytes=64)
+        scalar_cast(v_pool0[:], v_raw[0][:])
+        for lo, hi in ((0, NQ + 256), (NQ + 256, NQ + N)):
             nc.vector.quantize_mx(
-                out=k_codes[:, h * 256 : (h + 1) * 256].bitcast(FP8X4),
-                scales=k_scale[:, h * 256 : (h + 1) * 256],
-                in_=k_grp[:, h * 1024 : (h + 1) * 1024],
+                out=codes[:, lo:hi].bitcast(FP8X4), scales=scales[:, lo:hi], in_=grp[:, lo * 4 : hi * 4]
             )
 
-        nc.vector.quantize_mx(out=q_codes[:].bitcast(FP8X4), scales=q_scale[:], in_=q_grp[:])
-        quantize_k(0)
-        quantize_k(1)
-
         s_t = keep.tile([P, 4, NQ], F32, name="s_t")
-        banks = []
-        for half in range(2):
-            bank = psum.tile([P, 2, NQ], F32, name="qk", tag="x")
-            for c2 in range(2):
-                c = 2 * half + c2
-                sl = slice(c * P, (c + 1) * P)
-                nc.tensor.matmul_mx(
-                    out=bank[:, c2, :],
-                    lhsT=k_codes[:, sl].bitcast(FP8X4),
-                    lhsT_scale=k_scale[:, sl],
-                    rhs=q_codes[:].bitcast(FP8X4),
-                    rhs_scale=q_scale[:],
-                    start=True,
-                    stop=True,
-                )
-            banks.append(bank)
         for c in range(4):
+            bank = psum.tile([P, NQ], F32, name="qk", tag="x" if c < 2 else "w")
+            sl = slice(NQ + c * P, NQ + (c + 1) * P)
+            nc.tensor.matmul_mx(
+                out=bank[:],
+                lhsT=codes[:, sl].bitcast(FP8X4),
+                lhsT_scale=scales[:, sl],
+                rhs=codes[:, :NQ].bitcast(FP8X4),
+                rhs_scale=scales[:, :NQ],
+                start=True,
+                stop=True,
+            )
             nc.scalar.activation(
-                out=s_t[:, c, :], in_=banks[c // 2][:, c % 2, :], func=ACT.Identity,
+                out=s_t[:, c, :], in_=bank[:], func=ACT.Identity,
                 scale=ks_col[:, c : c + 1], bias=kb_col[:, c : c + 1],
             )
 
-        v_g = []
-        for e in range(2):
-            g = keep.tile([P, N], F32, name=f"v_g{e}", tag="pair1" if e == 0 else "k_grp", align_bytes=64)
-            nc.vector.tensor_copy(g[:], v_raw[e][:].indirect(offsets[:]))
-            v_g.append(g)
-        v_grp = keep.tile([P, DV * 4], BF16, name="v_grp", align_bytes=64)
-        v_codes = keep.tile([P, DV], U32, name="v_codes", align_bytes=64)
-        v_scale = keep.tile([P, DV], U8, name="v_scale", align_bytes=64)
+        g_all = keep.tile([P, 2, N], F32, name="g_all", tag="grp", align_bytes=64)
+        gather_table(vs_row, g_all[:, 0, :])
+        gather_table(v_raw[1], g_all[:, 1, :])
+        v_g0 = keep.tile([P, N, 2], BF16, name="v_g0", tag="k1b")
+        nc.scalar.activation(out=v_g0[:, :, 0], in_=v_pool0[:].indirect(offsets[:]), func=ACT.Copy)
+        vs_bank = turn_table(g_all[:, 0, :], 4, "vs", "z")
+        vs_col = column(vs_bank, "vs", "k1a")
 
         s_banks = []
         for b in range(2):
@@ -169,25 +167,29 @@ def tile_attend_x_ks_bias_srt_kernel(tc, qT, kT, vT, ks, vs, kb, offs, out):
             for c in range(4):
                 nc.tensor.transpose(bank[:, c * P : (c + 1) * P], s_t[:, c, b * P : (b + 1) * P], ident[:])
             s_banks.append(bank)
-        v_banks = []
-        for e in range(2):
-            bank = psum.tile([P, 4, P], F32, name="v_t", tag="z")
-            for t in range(4):
-                nc.tensor.transpose(bank[:, t, :], v_g[e][:, t : N : 4], ident[:])
-            v_banks.append(bank)
+        v1_bank = turn_table(g_all[:, 1, :], 4, "v1", "z")
+        v0_bank = psum.tile([P, 4, P], BF16, name="v0_t", tag="z")
+        for t in range(4):
+            nc.tensor.transpose(v0_bank[:, t, :], v_g0[:, t : N : 4, 0], ident_bf16[:])
 
-        def value_copy(engine_copy, e):
-            engine_copy(
-                v_grp[:, e * 512 : (e + 1) * 512].rearrange("p (e t) -> p e t", t=4),
-                v_banks[e][:].rearrange("p t e -> p e t"),
-            )
-
-        value_copy(scalar_cast, 0)
         neg_ms = []
         for b in range(2):
-            neg_m = keep.tile([P, 1], F32, name=f"neg_m{b}")
+            neg_m = keep.tile([P, 1], F32, name=f"neg_m{b}", tag=f"neg_m{b}", align_bytes=64)
             nc.vector.tensor_reduce(out=neg_m[:], in_=s_banks[b][:], axis=AX.X, op=ALU.max, negate=True)
             neg_ms.append(neg_m)
+        v_codes = keep.tile([P, DV], U32, name="v_codes", align_bytes=64)
+        v_scale = keep.tile([P, DV], U8, name="v_scale", align_bytes=64)
+
+        def value_group(engine_copy, bank, e, tag):
+            v_grp = keep.tile([P, P * 4], BF16, name=f"v_grp{e}", tag=tag, align_bytes=64)
+            engine_copy(v_grp[:].rearrange("p (e t) -> p e t", t=4), bank[:].rearrange("p t e -> p e t"))
+            return v_grp
+
+        def quantize_values(v_grp, e):
+            cols = slice(e * P, (e + 1) * P)
+            nc.vector.quantize_mx(out=v_codes[:, cols].bitcast(FP8X4), scales=v_scale[:, cols], in_=v_grp[:])
+
+        quantize_values(value_group(nc.vector.tensor_copy, v0_bank, 0, "v_grp0"), 0)
         p_tiles = []
         l_tiles = []
         for b in range(2):
@@ -202,7 +204,7 @@ def tile_attend_x_ks_bias_srt_kernel(tc, qT, kT, vT, ks, vs, kb, offs, out):
             )
             p_tiles.append(p)
             l_tiles.append(l)
-        value_copy(nc.vector.tensor_copy, 1)
+        v_grp1 = value_group(scalar_cast, v1_bank, 1, "neg_m1")
 
         for b in range(2):
             bank = psum.tile([P, 4, P], F32, name="p_t", tag="x")
@@ -219,7 +221,7 @@ def tile_attend_x_ks_bias_srt_kernel(tc, qT, kT, vT, ks, vs, kb, offs, out):
             w_scale = keep.tile([P, P], U8, name=f"w_scale{b}", align_bytes=64)
             nc.vector.quantize_mx(out=w_codes[:].bitcast(FP8X4), scales=w_scale[:], in_=w_grp[:])
             if b == 0:
-                nc.vector.quantize_mx(out=v_codes[:].bitcast(FP8X4), scales=v_scale[:], in_=v_grp[:])
+                quantize_values(v_grp1, 1)
             rl = keep.tile([P, 1], F32, name=f"rl{b}")
             nc.vector.reciprocal(rl[:], l_tiles[b][:])
             acc = psum.tile([P, DV], F32, name="acc", tag="w")

@@ -31,7 +31,6 @@ def tile_attend_x_ks_bias_srt_kernel(tc, qT, kT, vT, ks, vs, kb, offs, out):
         vs_row = keep.tile([P, T], F32, name="vs_row")
         warm = keep.tile([P, 1], F32, name="warm")
         ident = keep.tile([P, P], F32, name="ident")
-        ident_bf16 = keep.tile([P, P], BF16, name="ident_bf16")
 
         nc.sync.dma_start(offsets[:], offs)
         nc.vector.memset(warm[:], 0.0)
@@ -40,7 +39,6 @@ def tile_attend_x_ks_bias_srt_kernel(tc, qT, kT, vT, ks, vs, kb, offs, out):
             nc.gpsimd.memset(row[:, :cut], 0.0)
             nc.vector.memset(row[:, cut:], 0.0)
         make_identity(nc, ident[:])
-        make_identity(nc, ident_bf16[:])
 
         k_view = kT.rearrange("(p j) n -> p j n", j=4)
         k_pool = [keep.tile([P, T * 2], BF16, name=f"k_pool{u}", align_bytes=64) for u in range(2)]
@@ -74,12 +72,6 @@ def tile_attend_x_ks_bias_srt_kernel(tc, qT, kT, vT, ks, vs, kb, offs, out):
             nc.scalar.activation(out=col[:], in_=bank[:, :, 0], func=ACT.Copy)
             return col
 
-        def keep_tensor_engine_awake(blocks, tags):
-            for tag in tags:
-                bank = psum.tile([P, 4, P], F32, name="awake", tag=tag)
-                for i in range(4):
-                    nc.tensor.transpose(bank[:, i, :], blocks[:, i * P : (i + 1) * P], ident[:])
-
         k0a = load_pair(0, 0, 512, "k0a")
         nc.sync.dma_start(ks_row[0:1, :], ks[0:1, :])
         k0b = load_pair(0, 512, T, "k0b")
@@ -101,9 +93,6 @@ def tile_attend_x_ks_bias_srt_kernel(tc, qT, kT, vT, ks, vs, kb, offs, out):
         gather_table(kb_row, tab_g[:, 1, :])
         kb_bank = turn_table(tab_g[:, 1, :], 1, "kb", "x")
 
-        keep_tensor_engine_awake(k1a[:, 0, :], "yz")
-        keep_tensor_engine_awake(q_raw[:].rearrange("p j n -> p (j n)"), "yzyz")
-
         grp = keep.tile([P, (NQ + N) * 4], BF16, name="grp", tag="grp", align_bytes=64)
         codes = keep.tile([P, NQ + N], U32, name="codes", align_bytes=64)
         scales = keep.tile([P, NQ + N], U8, name="scales", align_bytes=64)
@@ -120,17 +109,14 @@ def tile_attend_x_ks_bias_srt_kernel(tc, qT, kT, vT, ks, vs, kb, offs, out):
                 k_words[:, h * 256 : (h + 1) * 256, 1],
                 k_pool[1][:].bitcast(U32).indirect(offsets[:, h * 16 : (h + 1) * 16]),
             )
-        q_half = NQ // 2
-        for engine_copy, lo in ((scalar_cast, 0), (nc.gpsimd.tensor_copy, q_half)):
+        for engine_copy, lo, hi in ((scalar_cast, 0, 160), (nc.vector.tensor_copy, 160, NQ)):
             engine_copy(
-                grp[:, 4 * lo : 4 * (lo + q_half)].rearrange("p (n j) -> p n j", j=4),
-                q_raw[:, :, lo : lo + q_half].rearrange("p j n -> p n j"),
+                grp[:, 4 * lo : 4 * hi].rearrange("p (n j) -> p n j", j=4),
+                q_raw[:, :, lo:hi].rearrange("p j n -> p n j"),
             )
         ks_col = column(ks_bank, "ks", "k1a")
         kb_col = column(kb_bank, "kb", "k1b")
-        v_pool0 = keep.tile([P, T], BF16, name="v_pool0", align_bytes=64)
-        scalar_cast(v_pool0[:], v_raw[0][:])
-        for lo, hi in ((0, NQ + 256), (NQ + 256, NQ + N)):
+        for lo, hi in ((NQ, NQ + 256), (NQ + 256, NQ + N), (0, NQ)):
             nc.vector.quantize_mx(
                 out=codes[:, lo:hi].bitcast(FP8X4), scales=scales[:, lo:hi], in_=grp[:, lo * 4 : hi * 4]
             )
@@ -153,11 +139,10 @@ def tile_attend_x_ks_bias_srt_kernel(tc, qT, kT, vT, ks, vs, kb, offs, out):
                 scale=ks_col[:, c : c + 1], bias=kb_col[:, c : c + 1],
             )
 
-        g_all = keep.tile([P, 2, N], F32, name="g_all", tag="grp", align_bytes=64)
+        g_all = keep.tile([P, 3, N], F32, name="g_all", tag="grp", align_bytes=64)
         gather_table(vs_row, g_all[:, 0, :])
-        gather_table(v_raw[1], g_all[:, 1, :])
-        v_g0 = keep.tile([P, N, 2], BF16, name="v_g0", tag="k1b")
-        nc.scalar.activation(out=v_g0[:, :, 0], in_=v_pool0[:].indirect(offsets[:]), func=ACT.Copy)
+        for e in range(2):
+            gather_table(v_raw[e], g_all[:, 1 + e, :])
         vs_bank = turn_table(g_all[:, 0, :], 4, "vs", "z")
         vs_col = column(vs_bank, "vs", "k1a")
 
@@ -167,10 +152,7 @@ def tile_attend_x_ks_bias_srt_kernel(tc, qT, kT, vT, ks, vs, kb, offs, out):
             for c in range(4):
                 nc.tensor.transpose(bank[:, c * P : (c + 1) * P], s_t[:, c, b * P : (b + 1) * P], ident[:])
             s_banks.append(bank)
-        v1_bank = turn_table(g_all[:, 1, :], 4, "v1", "z")
-        v0_bank = psum.tile([P, 4, P], BF16, name="v0_t", tag="z")
-        for t in range(4):
-            nc.tensor.transpose(v0_bank[:, t, :], v_g0[:, t : N : 4, 0], ident_bf16[:])
+        v_banks = [turn_table(g_all[:, 1 + e, :], 4, f"v{e}", "z") for e in range(2)]
 
         neg_ms = []
         for b in range(2):
@@ -189,7 +171,7 @@ def tile_attend_x_ks_bias_srt_kernel(tc, qT, kT, vT, ks, vs, kb, offs, out):
             cols = slice(e * P, (e + 1) * P)
             nc.vector.quantize_mx(out=v_codes[:, cols].bitcast(FP8X4), scales=v_scale[:, cols], in_=v_grp[:])
 
-        quantize_values(value_group(nc.vector.tensor_copy, v0_bank, 0, "v_grp0"), 0)
+        quantize_values(value_group(nc.vector.tensor_copy, v_banks[0], 0, "v_grp0"), 0)
         p_tiles = []
         l_tiles = []
         for b in range(2):
@@ -204,7 +186,7 @@ def tile_attend_x_ks_bias_srt_kernel(tc, qT, kT, vT, ks, vs, kb, offs, out):
             )
             p_tiles.append(p)
             l_tiles.append(l)
-        v_grp1 = value_group(scalar_cast, v1_bank, 1, "neg_m1")
+        v_grp1 = value_group(scalar_cast, v_banks[1], 1, "neg_m1")
 
         for b in range(2):
             bank = psum.tile([P, 4, P], F32, name="p_t", tag="x")

@@ -109,11 +109,7 @@ def tile_attend_x_ks_bias_srt_kernel(tc, qT, kT, vT, ks, vs, kb, offs, out):
                 k_words[:, h * 256 : (h + 1) * 256, 1],
                 k_pool[1][:].bitcast(U32).indirect(offsets[:, h * 16 : (h + 1) * 16]),
             )
-        for engine_copy, lo, hi in ((scalar_cast, 0, 160), (nc.vector.tensor_copy, 160, NQ)):
-            engine_copy(
-                grp[:, 4 * lo : 4 * hi].rearrange("p (n j) -> p n j", j=4),
-                q_raw[:, :, lo:hi].rearrange("p j n -> p n j"),
-            )
+        scalar_cast(grp[:, : NQ * 4].rearrange("p (n j) -> p n j", j=4), q_raw[:].rearrange("p j n -> p n j"))
         ks_col = column(ks_bank, "ks", "k1a")
         kb_col = column(kb_bank, "kb", "k1b")
         for lo, hi in ((NQ, NQ + 256), (NQ + 256, NQ + N), (0, NQ)):

from contextlib import ExitStack

import concourse.mybir as mybir
from concourse.masks import make_identity

P = 128
D, T, N, NQ, DV = 512, 1024, 512, 256, 256
F32 = mybir.dt.float32
BF16 = mybir.dt.bfloat16
U32 = mybir.dt.uint32
U16 = mybir.dt.uint16
U8 = mybir.dt.uint8
FP8X4 = mybir.dt.float8_e4m3fn_x4
ACT = mybir.ActivationFunctionType
ALU = mybir.AluOpType
AX = mybir.AxisListType

FLOPS = 2 * NQ * N * (D + DV)
BYTES = 4 * (D * NQ + (D + DV) * N + 3 * N + NQ * DV) + 2 * N


def tile_attend_x_ks_bias_srt_kernel(tc, qT, kT, vT, ks, vs, kb, offs, out):
    nc = tc.nc
    with ExitStack() as ctx:
        keep = ctx.enter_context(tc.tile_pool(name="keep", bufs=1))
        psum = ctx.enter_context(tc.psum_pool(name="psum", bufs=2))

        offsets = keep.tile([P, N // 16], U16, name="offsets")
        ks_row = keep.tile([P, T], F32, name="ks_row")
        kb_row = keep.tile([P, T], F32, name="kb_row")
        vs_row = keep.tile([P, T], F32, name="vs_row")
        warm = keep.tile([P, 1], F32, name="warm")
        ident = keep.tile([P, P], F32, name="ident")

        nc.sync.dma_start(offsets[:], offs)
        nc.vector.memset(warm[:], 0.0)
        nc.scalar.activation(out=warm[:], in_=warm[:], func=ACT.Exp)
        for row, cut in ((ks_row, 808), (kb_row, 512), (vs_row, 384)):
            nc.gpsimd.memset(row[:, :cut], 0.0)
            nc.vector.memset(row[:, cut:], 0.0)
        make_identity(nc, ident[:])

        k_view = kT.rearrange("(p j) n -> p j n", j=4)
        k_pool = [keep.tile([P, T * 2], BF16, name=f"k_pool{u}", align_bytes=64) for u in range(2)]

        def load_pair(j, lo, hi, name):
            t = keep.tile([P, 2, hi - lo], F32, name=name, tag=name)
            nc.sync.dma_start(t[:], k_view[:, j : j + 2, lo:hi])
            return t

        def cast_pair(engine_copy, pool, raw, lo, hi, base):
            engine_copy(
                pool[:, 2 * lo : 2 * hi].rearrange("p (n h) -> p n h", h=2),
                raw[:, :, lo - base : hi - base].rearrange("p h n -> p n h"),
            )

        def scalar_cast(o, i):
            nc.scalar.activation(out=o, in_=i, func=ACT.Copy)

        def gather_table(row, g):
            nc.vector.tensor_copy(g, row[:].indirect(offsets[:]))

        def turn_table(g, step, name, tag):
            bank = psum.tile([P, 4, P], F32, name=name + "_t", tag=tag)
            for c in range(4):
                src = g[:, c * P : (c + 1) * P] if step == 1 else g[:, c : N : 4]
                nc.tensor.transpose(bank[:, c, :], src, ident[:])
            return bank

        def column(bank, name, tag):
            col = keep.tile([P, 4], F32, name=name + "_c", tag=tag)
            nc.scalar.activation(out=col[:], in_=bank[:, :, 0], func=ACT.Copy)
            return col

        k0a = load_pair(0, 0, 512, "k0a")
        nc.sync.dma_start(ks_row[0:1, :], ks[0:1, :])
        k0b = load_pair(0, 512, T, "k0b")
        nc.sync.dma_start(kb_row[0:1, :], kb[0:1, :])
        k1a = load_pair(2, 0, 512, "k1a")
        k1b = load_pair(2, 512, T, "k1b")
        q_raw = keep.tile([P, 4, NQ], F32, name="q_raw", tag="q_raw")
        nc.sync.dma_start(q_raw[:], qT[0].rearrange("(p j) n -> p j n", j=4))
        nc.sync.dma_start(vs_row[0:1, :], vs[0:1, :])
        v_raw = []
        for e in range(2):
            t = keep.tile([P, T], F32, name=f"v_raw{e}")
            nc.sync.dma_start(t[:], vT[e * P : (e + 1) * P, :])
            v_raw.append(t)

        tab_g = keep.tile([P, 2, N], F32, name="tab_g", align_bytes=64)
        gather_table(ks_row, tab_g[:, 0, :])
        ks_bank = turn_table(tab_g[:, 0, :], 1, "ks", "x")
        gather_table(kb_row, tab_g[:, 1, :])
        kb_bank = turn_table(tab_g[:, 1, :], 1, "kb", "x")

        grp = keep.tile([P, (NQ + N) * 4], BF16, name="grp", tag="grp", align_bytes=64)
        codes = keep.tile([P, NQ + N], U32, name="codes", align_bytes=64)
        scales = keep.tile([P, NQ + N], U8, name="scales", align_bytes=64)
        k_words = grp[:, NQ * 4 :].bitcast(U32).rearrange("p (i u) -> p i u", u=2)

        cast_pair(scalar_cast, k_pool[0], k0a, 0, 512, 0)
        cast_pair(scalar_cast, k_pool[0], k0b, 512, T, 512)
        nc.vector.tensor_copy(k_words[:, :, 0], k_pool[0][:].bitcast(U32).indirect(offsets[:]))
        cast_pair(scalar_cast, k_pool[1], k1a, 0, 512, 0)
        cast_pair(scalar_cast, k_pool[1], k1b, 512, 704, 512)
        cast_pair(nc.vector.tensor_copy, k_pool[1], k1b, 704, T, 512)
        for h in range(2):
            nc.vector.tensor_copy(
                k_words[:, h * 256 : (h + 1) * 256, 1],
                k_pool[1][:].bitcast(U32).indirect(offsets[:, h * 16 : (h + 1) * 16]),
            )
        scalar_cast(grp[:, : NQ * 4].rearrange("p (n j) -> p n j", j=4), q_raw[:].rearrange("p j n -> p n j"))
        ks_col = column(ks_bank, "ks", "k1a")
        kb_col = column(kb_bank, "kb", "k1b")
        for lo, hi in ((NQ, NQ + 256), (NQ + 256, NQ + N), (0, NQ)):
            nc.vector.quantize_mx(
                out=codes[:, lo:hi].bitcast(FP8X4), scales=scales[:, lo:hi], in_=grp[:, lo * 4 : hi * 4]
            )

        s_t = keep.tile([P, 4, NQ], F32, name="s_t")
        for c in range(4):
            bank = psum.tile([P, NQ], F32, name="qk", tag="x" if c < 2 else "w")
            sl = slice(NQ + c * P, NQ + (c + 1) * P)
            nc.tensor.matmul_mx(
                out=bank[:],
                lhsT=codes[:, sl].bitcast(FP8X4),
                lhsT_scale=scales[:, sl],
                rhs=codes[:, :NQ].bitcast(FP8X4),
                rhs_scale=scales[:, :NQ],
                start=True,
                stop=True,
            )
            nc.scalar.activation(
                out=s_t[:, c, :], in_=bank[:], func=ACT.Identity,
                scale=ks_col[:, c : c + 1], bias=kb_col[:, c : c + 1],
            )

        g_all = keep.tile([P, 3, N], F32, name="g_all", tag="grp", align_bytes=64)
        gather_table(vs_row, g_all[:, 0, :])
        for e in range(2):
            gather_table(v_raw[e], g_all[:, 1 + e, :])
        vs_bank = turn_table(g_all[:, 0, :], 4, "vs", "z")
        vs_col = column(vs_bank, "vs", "k1a")

        s_banks = []
        for b in range(2):
            bank = psum.tile([P, N], F32, name="s_b", tag="y")
            for c in range(4):
                nc.tensor.transpose(bank[:, c * P : (c + 1) * P], s_t[:, c, b * P : (b + 1) * P], ident[:])
            s_banks.append(bank)
        v_banks = [turn_table(g_all[:, 1 + e, :], 4, f"v{e}", "z") for e in range(2)]

        neg_ms = []
        for b in range(2):
            neg_m = keep.tile([P, 1], F32, name=f"neg_m{b}", tag=f"neg_m{b}", align_bytes=64)
            nc.vector.tensor_reduce(out=neg_m[:], in_=s_banks[b][:], axis=AX.X, op=ALU.max, negate=True)
            neg_ms.append(neg_m)
        v_codes = keep.tile([P, DV], U32, name="v_codes", align_bytes=64)
        v_scale = keep.tile([P, DV], U8, name="v_scale", align_bytes=64)

        def value_group(engine_copy, bank, e, tag):
            v_grp = keep.tile([P, P * 4], BF16, name=f"v_grp{e}", tag=tag, align_bytes=64)
            engine_copy(v_grp[:].rearrange("p (e t) -> p e t", t=4), bank[:].rearrange("p t e -> p e t"))
            return v_grp

        def quantize_values(v_grp, e):
            cols = slice(e * P, (e + 1) * P)
            nc.vector.quantize_mx(out=v_codes[:, cols].bitcast(FP8X4), scales=v_scale[:, cols], in_=v_grp[:])

        quantize_values(value_group(nc.vector.tensor_copy, v_banks[0], 0, "v_grp0"), 0)
        p_tiles = []
        l_tiles = []
        for b in range(2):
            p = keep.tile([P, 4, P], F32, name=f"p{b}")
            l = keep.tile([P, 1], F32, name=f"l{b}")
            nc.scalar.activation(
                out=p[:],
                in_=s_banks[b][:].rearrange("p (s t) -> p t s", t=4),
                func=ACT.Exp,
                bias=neg_ms[b][:],
                accum_out=l[:],
            )
            p_tiles.append(p)
            l_tiles.append(l)
        v_grp1 = value_group(scalar_cast, v_banks[1], 1, "neg_m1")

        for b in range(2):
            bank = psum.tile([P, 4, P], F32, name="p_t", tag="x")
            for t in range(4):
                nc.tensor.transpose(bank[:, t, :], p_tiles[b][:, t, :], ident[:])
            w_grp = keep.tile([P, P * 4], BF16, name=f"w_grp{b}", align_bytes=64)
            nc.vector.tensor_tensor(
                out=w_grp[:].rearrange("p (q t) -> p q t", t=4),
                in0=bank[:].rearrange("p t q -> p q t"),
                in1=vs_col[:].unsqueeze(1).to_broadcast([P, P, 4]),
                op=ALU.mult,
            )
            w_codes = keep.tile([P, P], U32, name=f"w_codes{b}", align_bytes=64)
            w_scale = keep.tile([P, P], U8, name=f"w_scale{b}", align_bytes=64)
            nc.vector.quantize_mx(out=w_codes[:].bitcast(FP8X4), scales=w_scale[:], in_=w_grp[:])
            if b == 0:
                quantize_values(v_grp1, 1)
            rl = keep.tile([P, 1], F32, name=f"rl{b}")
            nc.vector.reciprocal(rl[:], l_tiles[b][:])
            acc = psum.tile([P, DV], F32, name="acc", tag="w")
            nc.tensor.matmul_mx(
                out=acc[:],
                lhsT=w_codes[:].bitcast(FP8X4),
                lhsT_scale=w_scale[:],
                rhs=v_codes[:].bitcast(FP8X4),
                rhs_scale=v_scale[:],
                start=True,
                stop=True,
            )
            y = keep.tile([P, DV], F32, name=f"y{b}")
            nc.scalar.activation(out=y[:], in_=acc[:], func=ACT.Copy, scale=rl[:])
            nc.sync.dma_start(out[0, b * P : (b + 1) * P, :], y[:])
